import numpy as np
import ml_dtypes

BF16 = ml_dtypes.bfloat16


def bf(x):
    return np.asarray(x, np.float32).astype(BF16)


def f32(x):
    return np.asarray(x, np.float32)


def f64(x):
    return np.asarray(x).astype(np.float64)


def striped(idx):
    return np.tile(idx.reshape(-1, 16).T, (8, 1))


S, K, M, N, D, V = 4096, 256, 128, 2048, 4, 512


def setup_inputs():
    return {"table": bf(np.random.standard_normal((K, S))), "w": bf(np.random.standard_normal((K, M)) / np.sqrt(D * K)), "b": f32(0.5 * np.random.standard_normal((M, 1))), "offs": striped(np.random.permutation(S)[:N])}


def reference(table, w, b, offs):
    idx = offs[:16].T.reshape(-1)
    x = f64(table)[:, idx]
    y = f64(w).T @ sum(x[:, t * V : (t + 1) * V] for t in range(D))
    return np.tanh(y + f64(b))

import concourse.mybir as mybir

BF16, F32, U16 = mybir.dt.bfloat16, mybir.dt.float32, mybir.dt.uint16
TANH = mybir.ActivationFunctionType.Tanh

P = 128
S, K, M = 4096, 256, 128
V, D = 512, 4
BLOCKS = K // P
PIECE = V // 16

FLOPS = 2 * K * M * V + (D - 1) * K * V


def tile_gather_matmul_kernel(tc, table, w, b, offs, out):
    nc = tc.nc
    with (
        tc.tile_pool(name="held", bufs=1) as held,
        tc.psum_pool(name="psum", bufs=1) as psum,
    ):
        offsets = held.tile([P, D * PIECE], U16, name="offsets")
        nc.sync.dma_start(offsets[:], offs)
        blocks = []
        for c in range(BLOCKS):
            block = held.tile([P, S], BF16, name=f"block{c}")
            nc.sync.dma_start(block[:], table[c * P : (c + 1) * P, :])
            blocks.append(block)

        weights = held.tile([P, BLOCKS, M], BF16, name="weights")
        nc.scalar.dma_start(weights[:], w.rearrange("(c p) m -> p c m", p=P))
        bias = held.tile([P, 1], F32, name="bias")
        nc.scalar.dma_start(bias[:], b)

        sums = psum.tile([P, V], F32, name="sums")
        for c in range(BLOCKS):
            for t in range(D):
                picked = blocks[c][:].indirect(offsets[:, t * PIECE : (t + 1) * PIECE])
                nc.tensor.matmul(
                    sums[:],
                    weights[:, c, :],
                    picked,
                    start=(c == 0 and t == 0),
                    stop=(c == BLOCKS - 1 and t == D - 1),
                )

        result = held.tile([P, V], F32, name="result")
        nc.scalar.activation(result[:], sums[:], TANH, bias=bias[:])
        nc.sync.dma_start(out, result[:])
